import numpy as np
import ml_dtypes


def mxq(x, axis, fmt="e4m3"):
    dtype, down = {"e4m3": (ml_dtypes.float8_e4m3fn, 7), "e5m2": (ml_dtypes.float8_e5m2, 14)}[fmt]
    v = np.moveaxis(np.asarray(x, np.float32).astype(ml_dtypes.bfloat16).astype(np.float64), axis, -1)
    blocks = v.reshape(v.shape[:-1] + (-1, 32))
    amax = np.abs(blocks).max(-1, keepdims=True)
    byte = np.maximum(np.where(amax > 0, np.frexp(amax)[1] - 1 + 127, 0) - down, 1)
    scale = np.exp2(byte - 127.0)
    codes = (blocks / scale).astype(np.float32).astype(dtype).astype(np.float64)
    return np.moveaxis((codes * scale).reshape(v.shape), -1, axis)


WIDE = False


def mx_kscale(k):
    if not WIDE:
        return np.ones(k)
    levels = np.array([10, -10, 5, -5, 0])
    if k % 512:
        return np.exp2(np.random.permutation(np.resize(levels, k // 32))).repeat(32)
    a = np.empty((k // 512, 16))
    for p in range(k // 512):
        a[p, :8] = np.random.permutation(np.resize(levels, 8))
        for g in range(8):
            far = levels[np.abs(levels - a[p, g]) >= 10]
            a[p, g + 8] = far[np.random.randint(len(far))]
    return np.exp2(a.ravel()).repeat(32)


def f64(x):
    return np.asarray(x).astype(np.float64)


def striped8(idx):
    return np.asarray(idx).reshape(8, -1, 16).transpose(0, 2, 1).reshape(128, -1).astype(np.uint16)


def unstriped8(offs):
    return offs.reshape(8, 16, -1).transpose(0, 2, 1).reshape(8, -1).astype(np.int64)


def pick8(x, idx, run):
    r = np.arange(len(x))
    return x[r[:, None], idx[r % (8 * run) // run]]


E2M1 = np.array([0.0, 0.5, 1.0, 1.5, 2.0, 3.0, 4.0, 6.0, -0.0, -0.5, -1.0, -1.5, -2.0, -3.0, -4.0, -6.0])


def pack_weight(w, fmt):
    k, n = w.shape
    w = f64(np.asarray(w, np.float32).astype(ml_dtypes.bfloat16)).reshape(k // 32, 32, n)
    amax = np.abs(w).max(1)
    if fmt == "e4m3":
        byte = np.frexp(amax)[1] - 1 + 127 - 7
    else:
        mant, ex = np.frexp(amax / 6.0)
        byte = np.where(mant > 0.5, ex, ex - 1) + 127
    byte = np.clip(np.where(amax > 0, byte, 1), 1, 254)
    scaled = (w * np.exp2(127.0 - byte)[:, None, :]).reshape(k, n).astype(np.float32)
    by_word = np.ascontiguousarray(scaled.reshape(k // 512, 128, 4, n).transpose(0, 1, 3, 2))
    if fmt == "e4m3":
        words = by_word.astype(ml_dtypes.float8_e4m3fn).view(np.uint8)
    else:
        c = by_word.astype(ml_dtypes.float4_e2m1fn).view(np.uint8) & 0xF
        words = (c[..., 0::2] | (c[..., 1::2] << 4)).reshape(k // 512, 128, 2 * n)
    return np.ascontiguousarray(words), np.ascontiguousarray(byte.astype(np.uint8).reshape(k // 512, 16, n))


def unpack_weight(words, scales, fmt):
    g, _, n = scales.shape
    words = np.ascontiguousarray(words).reshape(g, 128, n, -1)
    if fmt == "e4m3":
        vals = words.view(ml_dtypes.float8_e4m3fn).astype(np.float64)
    else:
        nib = np.empty((g, 128, n, 4), np.uint8)
        nib[..., 0::2] = words & 0xF
        nib[..., 1::2] = words >> 4
        vals = E2M1[nib]
    vals = vals * np.repeat(np.exp2(scales.astype(np.float64) - 127.0), 8, axis=1)[..., None]
    return vals.transpose(0, 1, 3, 2).reshape(g * 512, n)


def sigmoid(v):
    return 1.0 / (1.0 + np.exp(-v))


K, T, J, L, N = 512, 1024, 512, 512, 512


def setup_inputs():
    n = np.random.standard_normal
    idx = np.stack([np.random.permutation(T)[:J] for _ in range(8)])
    fk = mx_kscale(K)
    fl = mx_kscale(L)
    xtp = pack_weight(n((K, T)) / fk[:, None], "e4m3")
    wp = pack_weight(n((K, N)) * 1 / np.sqrt(K) * fk[:, None], "e2m1")
    wsp = pack_weight(n((L, N)) * 1 / np.sqrt(L) * fl[:, None], "e4m3")
    return {
        "xt_words": xtp[0],
        "xt_scales": xtp[1],
        "w_words": wp[0],
        "w_scales": wp[1],
        "sx": (n((L, J)) / fl[:, None]).astype(np.float32),
        "ws_words": wsp[0],
        "ws_scales": wsp[1],
        "offs": striped8(idx),
    }


def reference(xt_words, xt_scales, w_words, w_scales, sx, ws_words, ws_scales, offs):
    idx = unstriped8(offs)
    xtu = unpack_weight(xt_words, xt_scales, "e4m3")
    wu = unpack_weight(w_words, w_scales, "e2m1")
    wsu = unpack_weight(ws_words, ws_scales, "e4m3")
    xtidxg = pick8(xtu, idx, 64)
    p = wu.T @ xtidxg
    sxq = mxq(f64(sx), 0, "e4m3")
    q = wsu.T @ sxq
    y = p * sigmoid(q)
    return y

@@ -1,0 +1,129 @@
+from contextlib import ExitStack
+
+import concourse.mybir as mybir
+
+K, T, J, L, N = 512, 1024, 512, 512, 512
+FLOPS = 2 * K * N * J + 2 * L * N * J
+
+F32 = mybir.dt.float32
+BF16 = mybir.dt.bfloat16
+I32 = mybir.dt.int32
+U32 = mybir.dt.uint32
+U16 = mybir.dt.uint16
+U8 = mybir.dt.uint8
+FP8X4 = mybir.dt.float8_e4m3fn_x4
+FP4X4 = mybir.dt.float4_e2m1fn_x4
+
+P = 128
+PACK = 4
+HALF = J // 2
+QUADS = 4
+
+
+def tile_moe_expert_heads_gated_kernel(
+    tc, xt_words, xt_scales, w_words, w_scales, sx, ws_words, ws_scales, offs, out
+):
+    nc = tc.nc
+    with ExitStack() as ctx:
+        keep = ctx.enter_context(tc.tile_pool(name="keep", bufs=1))
+        psum = ctx.enter_context(tc.psum_pool(name="psum", bufs=1))
+
+        lists = keep.tile([P, J // 16], U16, name="lists")
+        xs_window = keep.tile([P, T], U8, name="xs_window", align_bytes=64)
+        xw_window = keep.tile([P, T], I32, name="xw_window", align_bytes=64)
+        ws_plane = keep.tile([P, N], U8, name="ws_plane", align_bytes=64)
+        w_plane = keep.tile([P, N], U8, name="w_plane", align_bytes=64)
+        x_plane = keep.tile([P, J], U8, name="x_plane", align_bytes=64)
+        ws_codes = keep.tile([P, N], I32, name="ws_codes", align_bytes=64)
+        w_codes = keep.tile([P, 2 * N], U8, name="w_codes", align_bytes=64)
+        raw = [keep.tile([P, PACK, HALF], F32, name=f"raw{h}", align_bytes=64) for h in range(2)]
+
+        nc.vector.memset(x_plane[:].bitcast(I32)[96:P, :], 0)
+
+        def load_sx(h):
+            nc.sync.dma_start(
+                out=raw[h][:], in_=sx[:, h * HALF : (h + 1) * HALF].rearrange("(p t) j -> p t j", t=PACK)
+            )
+
+        def load_plane(plane, scales):
+            rows = scales[0].bitcast(I32)
+            for x in range(QUADS):
+                nc.sync.dma_start(
+                    out=plane[:].bitcast(I32)[32 * x : 32 * x + 32, :],
+                    in_=rows[4 * x : 4 * x + 4, :].unsqueeze(0).to_broadcast([8, 4, N // 4]),
+                )
+
+        nc.sync.dma_start(lists[:], offs)
+        xs_rows = xt_scales[0].bitcast(I32)
+        for c, queue in enumerate((nc.scalar, nc.sync)):
+            queue.dma_start(
+                out=xs_window[:].bitcast(I32)[c:P:2, :],
+                in_=xs_rows[c:16:2, :].unsqueeze(1).to_broadcast([8, 8, T // 4]),
+            )
+        load_sx(0)
+        nc.sync.dma_start(out=ws_codes[:], in_=ws_words[0].rearrange("p n t -> p (n t)").bitcast(I32))
+        load_plane(ws_plane, ws_scales)
+        load_sx(1)
+        nc.sync.dma_start(out=xw_window[:], in_=xt_words[0].rearrange("p n t -> p (n t)").bitcast(I32))
+        nc.sync.dma_start(out=w_codes[:].bitcast(I32), in_=w_words[0].bitcast(I32))
+        load_plane(w_plane, w_scales)
+
+        xs_picked = keep.tile([P, J], U8, name="xs_picked", align_bytes=64)
+        nc.vector.tensor_copy(xs_picked[:], xs_window[:].indirect(lists[:]))
+        nc.sync.dma_start(out=x_plane[:].bitcast(I32)[0:112, :], in_=xs_picked[:].bitcast(I32)[14:126, :])
+
+        gates = {}
+        for h in range(2):
+            grouped = keep.tile([P, HALF, PACK], BF16, name=f"grouped{h}", align_bytes=64)
+            nc.vector.tensor_copy(
+                out=grouped[:].rearrange("p (c i) t -> p c t i", i=4),
+                in_=raw[h][:].rearrange("p t (c i) -> p c t i", i=4),
+            )
+            sx_codes = keep.tile([P, HALF], U32, name=f"sx_codes{h}", align_bytes=64)
+            sx_plane = keep.tile([P, HALF], U8, name=f"sx_plane{h}", align_bytes=64)
+            nc.vector.quantize_mx(
+                out=sx_codes[:].bitcast(FP8X4), scales=sx_plane[:], in_=grouped[:].rearrange("p j t -> p (j t)")
+            )
+            for u in range(2):
+                q_bank = psum.tile([P, 2, HALF], F32, name=f"q{h}{u}")
+                for i in range(2):
+                    cols = slice((2 * u + i) * P, (2 * u + i + 1) * P)
+                    nc.tensor.matmul_mx(
+                        out=q_bank[:, i, :],
+                        lhsT=ws_codes[:, cols].bitcast(FP8X4),
+                        lhsT_scale=ws_plane[:, cols],
+                        rhs=sx_codes[:].bitcast(FP8X4),
+                        rhs_scale=sx_plane[:],
+                        start=True,
+                        stop=True,
+                    )
+                gate = keep.tile([P, 2, HALF], F32, name=f"gate{h}{u}")
+                nc.scalar.activation(out=gate[:], in_=q_bank[:], func=mybir.ActivationFunctionType.Sigmoid)
+                gates[h, u] = gate
+
+        out_rows = out.rearrange("(m p) j -> p m j", p=P)
+        picked = []
+        for h in range(2):
+            xw_picked = keep.tile([P, HALF], U32, name=f"xw_picked{h}", align_bytes=64)
+            nc.vector.tensor_copy(
+                xw_picked[:], xw_window[:].bitcast(U32).indirect(lists[:, h * (HALF // 16) : (h + 1) * (HALF // 16)])
+            )
+            picked.append(xw_picked)
+        for h in range(2):
+            xw_picked = picked[h]
+            for u in range(2):
+                p_bank = psum.tile([P, 2, HALF], F32, name=f"p{h}{u}")
+                for i in range(2):
+                    m = 2 * u + i
+                    nc.tensor.matmul_mx(
+                        out=p_bank[:, i, :],
+                        lhsT=w_codes[:, 2 * m * P : 2 * (m + 1) * P].bitcast(FP4X4),
+                        lhsT_scale=w_plane[:, m * P : (m + 1) * P],
+                        rhs=xw_picked[:].bitcast(FP8X4),
+                        rhs_scale=x_plane[:, h * HALF : (h + 1) * HALF],
+                        start=True,
+                        stop=True,
+                    )
+                result = keep.tile([P, 2, HALF], F32, name=f"result{h}{u}")
+                nc.vector.tensor_tensor(out=result[:], in0=p_bank[:], in1=gates[h, u][:], op=mybir.AluOpType.mult)
+                nc.sync.dma_start(out=out_rows[:, 2 * u : 2 * u + 2, h * HALF : (h + 1) * HALF], in_=result[:])

@@ -38,47 +38,54 @@ def tile_moe_expert_heads_gated_kernel(
         w_codes = keep.tile([P, 2 * N], U8, name="w_codes", align_bytes=64)
         raw = [keep.tile([P, PACK, HALF], F32, name=f"raw{h}", align_bytes=64) for h in range(2)]
 
-        nc.vector.memset(x_plane[:].bitcast(I32)[96:P, :], 0)
-
         def load_sx(h):
             nc.sync.dma_start(
                 out=raw[h][:], in_=sx[:, h * HALF : (h + 1) * HALF].rearrange("(p t) j -> p t j", t=PACK)
             )
 
-        def load_plane(plane, scales):
-            rows = scales[0].bitcast(I32)
-            for x in range(QUADS):
-                nc.sync.dma_start(
-                    out=plane[:].bitcast(I32)[32 * x : 32 * x + 32, :],
-                    in_=rows[4 * x : 4 * x + 4, :].unsqueeze(0).to_broadcast([8, 4, N // 4]),
-                )
-
         nc.sync.dma_start(lists[:], offs)
-        xs_rows = xt_scales[0].bitcast(I32)
-        for c, queue in enumerate((nc.scalar, nc.sync)):
-            queue.dma_start(
-                out=xs_window[:].bitcast(I32)[c:P:2, :],
-                in_=xs_rows[c:16:2, :].unsqueeze(1).to_broadcast([8, 8, T // 4]),
-            )
+        nc.scalar.dma_start(
+            out=xs_window[:].bitcast(I32), in_=xt_scales[0].bitcast(I32).unsqueeze(1).to_broadcast([16, 8, T // 4])
+        )
         load_sx(0)
+        ws_rows = ws_scales[0].bitcast(I32)
+        for x in range(QUADS):
+            nc.scalar.dma_start(
+                out=ws_plane[:].bitcast(I32)[32 * x : 32 * x + 32, :],
+                in_=ws_rows[4 * x : 4 * x + 4, :].unsqueeze(0).to_broadcast([8, 4, N // 4]),
+            )
         nc.sync.dma_start(out=ws_codes[:], in_=ws_words[0].rearrange("p n t -> p (n t)").bitcast(I32))
-        load_plane(ws_plane, ws_scales)
         load_sx(1)
         nc.sync.dma_start(out=xw_window[:], in_=xt_words[0].rearrange("p n t -> p (n t)").bitcast(I32))
         nc.sync.dma_start(out=w_codes[:].bitcast(I32), in_=w_words[0].bitcast(I32))
-        load_plane(w_plane, w_scales)
+        nc.gpsimd.memset(w_plane[:].bitcast(I32), 0)
+        w_rows = w_scales[0].bitcast(I32)
+        for x in range(QUADS):
+            nc.gpsimd.dma_start(out=w_plane[:].bitcast(I32)[32 * x : 32 * x + 4, :], in_=w_rows[4 * x : 4 * x + 4, :])
 
         xs_picked = keep.tile([P, J], U8, name="xs_picked", align_bytes=64)
         nc.vector.tensor_copy(xs_picked[:], xs_window[:].indirect(lists[:]))
-        nc.sync.dma_start(out=x_plane[:].bitcast(I32)[0:112, :], in_=xs_picked[:].bitcast(I32)[14:126, :])
 
-        gates = {}
-        for h in range(2):
+        gates, picked, p_banks = {}, {}, {}
+        out_rows = out.rearrange("(m p) j -> p m j", p=P)
+
+        def place_token_scales():
+            nc.vector.tensor_copy(x_plane[:].bitcast(I32), xs_picked[:].bitcast(I32))
+            for r in range(1, 4):
+                nc.sync.dma_start(
+                    out=x_plane[:].bitcast(I32)[r:P:32, :], in_=xs_picked[:].bitcast(I32)[8 * r : P : 32, :]
+                )
+
+        def gate_half(h, act_cols):
             grouped = keep.tile([P, HALF, PACK], BF16, name=f"grouped{h}", align_bytes=64)
-            nc.vector.tensor_copy(
-                out=grouped[:].rearrange("p (c i) t -> p c t i", i=4),
-                in_=raw[h][:].rearrange("p t (c i) -> p c t i", i=4),
-            )
+            for copy, cols in ((nc.scalar.copy, slice(0, act_cols)), (nc.vector.tensor_copy, slice(act_cols, HALF))):
+                if cols.stop > cols.start:
+                    copy(
+                        out=grouped[:, cols, :].rearrange("p (c i) t -> p c t i", i=4),
+                        in_=raw[h][:, :, cols].rearrange("p t (c i) -> p c t i", i=4),
+                    )
+            if h == 0:
+                place_token_scales()
             sx_codes = keep.tile([P, HALF], U32, name=f"sx_codes{h}", align_bytes=64)
             sx_plane = keep.tile([P, HALF], U8, name=f"sx_plane{h}", align_bytes=64)
             nc.vector.quantize_mx(
@@ -88,42 +95,37 @@ def tile_moe_expert_heads_gated_kernel(
                 q_bank = psum.tile([P, 2, HALF], F32, name=f"q{h}{u}")
                 for i in range(2):
                     cols = slice((2 * u + i) * P, (2 * u + i + 1) * P)
-                    nc.tensor.matmul_mx(
-                        out=q_bank[:, i, :],
-                        lhsT=ws_codes[:, cols].bitcast(FP8X4),
-                        lhsT_scale=ws_plane[:, cols],
-                        rhs=sx_codes[:].bitcast(FP8X4),
-                        rhs_scale=sx_plane[:],
-                        start=True,
-                        stop=True,
-                    )
+                    nc.tensor.matmul_mx(out=q_bank[:, i, :], lhsT=ws_codes[:, cols].bitcast(FP8X4), lhsT_scale=ws_plane[:, cols], rhs=sx_codes[:].bitcast(FP8X4), rhs_scale=sx_plane[:], start=True, stop=True)
                 gate = keep.tile([P, 2, HALF], F32, name=f"gate{h}{u}")
                 nc.scalar.activation(out=gate[:], in_=q_bank[:], func=mybir.ActivationFunctionType.Sigmoid)
                 gates[h, u] = gate
 
-        out_rows = out.rearrange("(m p) j -> p m j", p=P)
-        picked = []
-        for h in range(2):
-            xw_picked = keep.tile([P, HALF], U32, name=f"xw_picked{h}", align_bytes=64)
+        def pick_half(h):
+            picked[h] = keep.tile([P, HALF], U32, name=f"xw_picked{h}", align_bytes=64)
             nc.vector.tensor_copy(
-                xw_picked[:], xw_window[:].bitcast(U32).indirect(lists[:, h * (HALF // 16) : (h + 1) * (HALF // 16)])
+                picked[h][:], xw_window[:].bitcast(U32).indirect(lists[:, h * (HALF // 16) : (h + 1) * (HALF // 16)])
             )
-            picked.append(xw_picked)
-        for h in range(2):
-            xw_picked = picked[h]
+
+        def product_half(h):
             for u in range(2):
-                p_bank = psum.tile([P, 2, HALF], F32, name=f"p{h}{u}")
+                p_banks[h, u] = psum.tile([P, 2, HALF], F32, name=f"p{h}{u}")
                 for i in range(2):
                     m = 2 * u + i
-                    nc.tensor.matmul_mx(
-                        out=p_bank[:, i, :],
-                        lhsT=w_codes[:, 2 * m * P : 2 * (m + 1) * P].bitcast(FP4X4),
-                        lhsT_scale=w_plane[:, m * P : (m + 1) * P],
-                        rhs=xw_picked[:].bitcast(FP8X4),
-                        rhs_scale=x_plane[:, h * HALF : (h + 1) * HALF],
-                        start=True,
-                        stop=True,
-                    )
-                result = keep.tile([P, 2, HALF], F32, name=f"result{h}{u}")
-                nc.vector.tensor_tensor(out=result[:], in0=p_bank[:], in1=gates[h, u][:], op=mybir.AluOpType.mult)
-                nc.sync.dma_start(out=out_rows[:, 2 * u : 2 * u + 2, h * HALF : (h + 1) * HALF], in_=result[:])
+                    nc.tensor.matmul_mx(out=p_banks[h, u][:, i, :], lhsT=w_codes[:, 2 * m * P : 2 * (m + 1) * P].bitcast(FP4X4), lhsT_scale=w_plane[:, m * P : (m + 1) * P], rhs=picked[h][:].bitcast(FP8X4), rhs_scale=x_plane[:, h * HALF : (h + 1) * HALF], start=True, stop=True)
+
+        def finish(h, u, pieces):
+            result = keep.tile([P, 2, HALF], F32, name=f"result{h}{u}")
+            for i0, i1 in pieces:
+                nc.vector.tensor_tensor(out=result[:, i0:i1, :], in0=p_banks[h, u][:, i0:i1, :], in1=gates[h, u][:, i0:i1, :], op=mybir.AluOpType.mult)
+                nc.sync.dma_start(out=out_rows[:, 2 * u + i0 : 2 * u + i1, h * HALF : (h + 1) * HALF], in_=result[:, i0:i1, :])
+
+        gate_half(0, 0)
+        gate_half(1, 0)
+        pick_half(0)
+        pick_half(1)
+        product_half(0)
+        product_half(1)
+        finish(0, 0, [(0, 2)])
+        finish(0, 1, [(0, 2)])
+        finish(1, 0, [(0, 2)])
+        finish(1, 1, [(0, 1), (1, 2)])

@@ -43,30 +43,29 @@ def tile_moe_expert_heads_gated_kernel(
                 out=raw[h][:], in_=sx[:, h * HALF : (h + 1) * HALF].rearrange("(p t) j -> p t j", t=PACK)
             )
 
+        nc.vector.memset(ws_plane[:].bitcast(I32), 0)
         nc.sync.dma_start(lists[:], offs)
         nc.scalar.dma_start(
             out=xs_window[:].bitcast(I32), in_=xt_scales[0].bitcast(I32).unsqueeze(1).to_broadcast([16, 8, T // 4])
         )
         load_sx(0)
+        nc.sync.dma_start(out=ws_codes[:], in_=ws_words[0].rearrange("p n t -> p (n t)").bitcast(I32))
         ws_rows = ws_scales[0].bitcast(I32)
         for x in range(QUADS):
-            nc.scalar.dma_start(
-                out=ws_plane[:].bitcast(I32)[32 * x : 32 * x + 32, :],
-                in_=ws_rows[4 * x : 4 * x + 4, :].unsqueeze(0).to_broadcast([8, 4, N // 4]),
-            )
-        nc.sync.dma_start(out=ws_codes[:], in_=ws_words[0].rearrange("p n t -> p (n t)").bitcast(I32))
+            nc.sync.dma_start(out=ws_plane[:].bitcast(I32)[32 * x : 32 * x + 4, :], in_=ws_rows[4 * x : 4 * x + 4, :])
         load_sx(1)
         nc.sync.dma_start(out=xw_window[:], in_=xt_words[0].rearrange("p n t -> p (n t)").bitcast(I32))
         nc.sync.dma_start(out=w_codes[:].bitcast(I32), in_=w_words[0].bitcast(I32))
         nc.gpsimd.memset(w_plane[:].bitcast(I32), 0)
         w_rows = w_scales[0].bitcast(I32)
         for x in range(QUADS):
-            nc.gpsimd.dma_start(out=w_plane[:].bitcast(I32)[32 * x : 32 * x + 4, :], in_=w_rows[4 * x : 4 * x + 4, :])
+            queue = nc.gpsimd if x < 2 else nc.sync
+            queue.dma_start(out=w_plane[:].bitcast(I32)[32 * x : 32 * x + 4, :], in_=w_rows[4 * x : 4 * x + 4, :])
 
         xs_picked = keep.tile([P, J], U8, name="xs_picked", align_bytes=64)
         nc.vector.tensor_copy(xs_picked[:], xs_window[:].indirect(lists[:]))
 
-        gates, picked, p_banks = {}, {}, {}
+        gates, picked, p_banks, quantised = {}, {}, {}, {}
         out_rows = out.rearrange("(m p) j -> p m j", p=P)
 
         def place_token_scales():
@@ -91,13 +90,18 @@ def tile_moe_expert_heads_gated_kernel(
             nc.vector.quantize_mx(
                 out=sx_codes[:].bitcast(FP8X4), scales=sx_plane[:], in_=grouped[:].rearrange("p j t -> p (j t)")
             )
-            for u in range(2):
-                q_bank = psum.tile([P, 2, HALF], F32, name=f"q{h}{u}")
+            quantised[h] = (sx_codes, sx_plane)
+
+        def gate_pair(h, u, bank_tag, pieces):
+            sx_codes, sx_plane = quantised[h]
+            if True:
+                q_bank = psum.tile([P, 2, HALF], F32, name=f"q{h}{u}", tag=bank_tag)
                 for i in range(2):
                     cols = slice((2 * u + i) * P, (2 * u + i + 1) * P)
                     nc.tensor.matmul_mx(out=q_bank[:, i, :], lhsT=ws_codes[:, cols].bitcast(FP8X4), lhsT_scale=ws_plane[:, cols], rhs=sx_codes[:].bitcast(FP8X4), rhs_scale=sx_plane[:], start=True, stop=True)
                 gate = keep.tile([P, 2, HALF], F32, name=f"gate{h}{u}")
-                nc.scalar.activation(out=gate[:], in_=q_bank[:], func=mybir.ActivationFunctionType.Sigmoid)
+                for i0, i1 in pieces:
+                    nc.scalar.activation(out=gate[:, i0:i1, :], in_=q_bank[:, i0:i1, :], func=mybir.ActivationFunctionType.Sigmoid)
                 gates[h, u] = gate
 
         def pick_half(h):
@@ -106,26 +110,28 @@ def tile_moe_expert_heads_gated_kernel(
                 picked[h][:], xw_window[:].bitcast(U32).indirect(lists[:, h * (HALF // 16) : (h + 1) * (HALF // 16)])
             )
 
-        def product_half(h):
+        def product(h, ms, tag):
+            bank = psum.tile([P, len(ms), HALF], F32, name=f"p{h}{ms[0]}", tag=tag)
+            for i, m in enumerate(ms):
+                nc.tensor.matmul_mx(out=bank[:, i, :], lhsT=w_codes[:, 2 * m * P : 2 * (m + 1) * P].bitcast(FP4X4), lhsT_scale=w_plane[:, m * P : (m + 1) * P], rhs=picked[h][:].bitcast(FP8X4), rhs_scale=x_plane[:, h * HALF : (h + 1) * HALF], start=True, stop=True)
+            p_banks[h, ms[0]] = bank
+
+        def finish(h, ms):
+            m0, count = ms[0], len(ms)
+            result = keep.tile([P, count, HALF], F32, name=f"result{h}{m0}")
+            gate = gates[h, m0 // 2][:, m0 % 2 : m0 % 2 + count, :]
+            nc.vector.tensor_tensor(out=result[:], in0=p_banks[h, m0][:], in1=gate, op=mybir.AluOpType.mult)
+            nc.sync.dma_start(out=out_rows[:, m0 : m0 + count, h * HALF : (h + 1) * HALF], in_=result[:])
+
+        whole = [(0, 2)]
+        for h in range(2):
+            gate_half(h, 0)
             for u in range(2):
-                p_banks[h, u] = psum.tile([P, 2, HALF], F32, name=f"p{h}{u}")
-                for i in range(2):
-                    m = 2 * u + i
-                    nc.tensor.matmul_mx(out=p_banks[h, u][:, i, :], lhsT=w_codes[:, 2 * m * P : 2 * (m + 1) * P].bitcast(FP4X4), lhsT_scale=w_plane[:, m * P : (m + 1) * P], rhs=picked[h][:].bitcast(FP8X4), rhs_scale=x_plane[:, h * HALF : (h + 1) * HALF], start=True, stop=True)
-
-        def finish(h, u, pieces):
-            result = keep.tile([P, 2, HALF], F32, name=f"result{h}{u}")
-            for i0, i1 in pieces:
-                nc.vector.tensor_tensor(out=result[:, i0:i1, :], in0=p_banks[h, u][:, i0:i1, :], in1=gates[h, u][:, i0:i1, :], op=mybir.AluOpType.mult)
-                nc.sync.dma_start(out=out_rows[:, 2 * u + i0 : 2 * u + i1, h * HALF : (h + 1) * HALF], in_=result[:, i0:i1, :])
-
-        gate_half(0, 0)
-        gate_half(1, 0)
+                gate_pair(h, u, f"q{u}", whole)
         pick_half(0)
         pick_half(1)
-        product_half(0)
-        product_half(1)
-        finish(0, 0, [(0, 2)])
-        finish(0, 1, [(0, 2)])
-        finish(1, 0, [(0, 2)])
-        finish(1, 1, [(0, 1), (1, 2)])
+        pieces = [(0, [0]), (0, [1]), (0, [2, 3]), (1, [0, 1]), (1, [2]), (1, [3])]
+        for h, ms in pieces:
+            product(h, ms, f"p{h}{ms[0]}")
+        for h, ms in pieces:
+            finish(h, ms)

@@ -45,7 +45,7 @@ def tile_moe_expert_heads_gated_kernel(
 
         nc.vector.memset(ws_plane[:].bitcast(I32), 0)
         nc.sync.dma_start(lists[:], offs)
-        nc.scalar.dma_start(
+        nc.sync.dma_start(
             out=xs_window[:].bitcast(I32), in_=xt_scales[0].bitcast(I32).unsqueeze(1).to_broadcast([16, 8, T // 4])
         )
         load_sx(0)
@@ -59,8 +59,7 @@ def tile_moe_expert_heads_gated_kernel(
         nc.gpsimd.memset(w_plane[:].bitcast(I32), 0)
         w_rows = w_scales[0].bitcast(I32)
         for x in range(QUADS):
-            queue = nc.gpsimd if x < 2 else nc.sync
-            queue.dma_start(out=w_plane[:].bitcast(I32)[32 * x : 32 * x + 4, :], in_=w_rows[4 * x : 4 * x + 4, :])
+            nc.gpsimd.dma_start(out=w_plane[:].bitcast(I32)[32 * x : 32 * x + 4, :], in_=w_rows[4 * x : 4 * x + 4, :])
 
         xs_picked = keep.tile([P, J], U8, name="xs_picked", align_bytes=64)
         nc.vector.tensor_copy(xs_picked[:], xs_window[:].indirect(lists[:]))
@@ -114,13 +113,15 @@ def tile_moe_expert_heads_gated_kernel(
             bank = psum.tile([P, len(ms), HALF], F32, name=f"p{h}{ms[0]}", tag=tag)
             for i, m in enumerate(ms):
                 nc.tensor.matmul_mx(out=bank[:, i, :], lhsT=w_codes[:, 2 * m * P : 2 * (m + 1) * P].bitcast(FP4X4), lhsT_scale=w_plane[:, m * P : (m + 1) * P], rhs=picked[h][:].bitcast(FP8X4), rhs_scale=x_plane[:, h * HALF : (h + 1) * HALF], start=True, stop=True)
-            p_banks[h, ms[0]] = bank
+            for i, m in enumerate(ms):
+                p_banks[h, m] = (bank, i)
 
         def finish(h, ms):
             m0, count = ms[0], len(ms)
             result = keep.tile([P, count, HALF], F32, name=f"result{h}{m0}")
+            bank, i0 = p_banks[h, m0]
             gate = gates[h, m0 // 2][:, m0 % 2 : m0 % 2 + count, :]
-            nc.vector.tensor_tensor(out=result[:], in0=p_banks[h, m0][:], in1=gate, op=mybir.AluOpType.mult)
+            nc.vector.tensor_tensor(out=result[:], in0=bank[:, i0 : i0 + count, :], in1=gate, op=mybir.AluOpType.mult)
             nc.sync.dma_start(out=out_rows[:, m0 : m0 + count, h * HALF : (h + 1) * HALF], in_=result[:])
 
         whole = [(0, 2)]
@@ -133,5 +134,5 @@ def tile_moe_expert_heads_gated_kernel(
         pieces = [(0, [0]), (0, [1]), (0, [2, 3]), (1, [0, 1]), (1, [2]), (1, [3])]
         for h, ms in pieces:
             product(h, ms, f"p{h}{ms[0]}")
-        for h, ms in pieces:
+        for h, ms in [(0, [0]), (0, [1]), (0, [2]), (0, [3]), (1, [0, 1]), (1, [2]), (1, [3])]:
             finish(h, ms)

from contextlib import ExitStack

import concourse.mybir as mybir

K, T, J, L, N = 512, 1024, 512, 512, 512
FLOPS = 2 * K * N * J + 2 * L * N * J

F32 = mybir.dt.float32
BF16 = mybir.dt.bfloat16
I32 = mybir.dt.int32
U32 = mybir.dt.uint32
U16 = mybir.dt.uint16
U8 = mybir.dt.uint8
FP8X4 = mybir.dt.float8_e4m3fn_x4
FP4X4 = mybir.dt.float4_e2m1fn_x4

P = 128
PACK = 4
HALF = J // 2
QUADS = 4


def tile_moe_expert_heads_gated_kernel(
    tc, xt_words, xt_scales, w_words, w_scales, sx, ws_words, ws_scales, offs, out
):
    nc = tc.nc
    with ExitStack() as ctx:
        keep = ctx.enter_context(tc.tile_pool(name="keep", bufs=1))
        psum = ctx.enter_context(tc.psum_pool(name="psum", bufs=1))

        lists = keep.tile([P, J // 16], U16, name="lists")
        xs_window = keep.tile([P, T], U8, name="xs_window", align_bytes=64)
        xw_window = keep.tile([P, T], I32, name="xw_window", align_bytes=64)
        ws_plane = keep.tile([P, N], U8, name="ws_plane", align_bytes=64)
        w_plane = keep.tile([P, N], U8, name="w_plane", align_bytes=64)
        x_plane = keep.tile([P, J], U8, name="x_plane", align_bytes=64)
        ws_codes = keep.tile([P, N], I32, name="ws_codes", align_bytes=64)
        w_codes = keep.tile([P, 2 * N], U8, name="w_codes", align_bytes=64)
        raw = [keep.tile([P, PACK, HALF], F32, name=f"raw{h}", align_bytes=64) for h in range(2)]

        def load_sx(h):
            nc.sync.dma_start(
                out=raw[h][:], in_=sx[:, h * HALF : (h + 1) * HALF].rearrange("(p t) j -> p t j", t=PACK)
            )

        nc.vector.memset(ws_plane[:].bitcast(I32), 0)
        nc.sync.dma_start(lists[:], offs)
        nc.sync.dma_start(
            out=xs_window[:].bitcast(I32), in_=xt_scales[0].bitcast(I32).unsqueeze(1).to_broadcast([16, 8, T // 4])
        )
        load_sx(0)
        nc.sync.dma_start(out=ws_codes[:], in_=ws_words[0].rearrange("p n t -> p (n t)").bitcast(I32))
        ws_rows = ws_scales[0].bitcast(I32)
        for x in range(QUADS):
            nc.sync.dma_start(out=ws_plane[:].bitcast(I32)[32 * x : 32 * x + 4, :], in_=ws_rows[4 * x : 4 * x + 4, :])
        load_sx(1)
        nc.sync.dma_start(out=xw_window[:], in_=xt_words[0].rearrange("p n t -> p (n t)").bitcast(I32))
        nc.sync.dma_start(out=w_codes[:].bitcast(I32), in_=w_words[0].bitcast(I32))
        nc.gpsimd.memset(w_plane[:].bitcast(I32), 0)
        w_rows = w_scales[0].bitcast(I32)
        for x in range(QUADS):
            nc.gpsimd.dma_start(out=w_plane[:].bitcast(I32)[32 * x : 32 * x + 4, :], in_=w_rows[4 * x : 4 * x + 4, :])

        xs_picked = keep.tile([P, J], U8, name="xs_picked", align_bytes=64)
        nc.vector.tensor_copy(xs_picked[:], xs_window[:].indirect(lists[:]))

        gates, picked, p_banks, quantised = {}, {}, {}, {}
        out_rows = out.rearrange("(m p) j -> p m j", p=P)

        def place_token_scales():
            nc.vector.tensor_copy(x_plane[:].bitcast(I32), xs_picked[:].bitcast(I32))
            for r in range(1, 4):
                nc.sync.dma_start(
                    out=x_plane[:].bitcast(I32)[r:P:32, :], in_=xs_picked[:].bitcast(I32)[8 * r : P : 32, :]
                )

        def gate_half(h, act_cols):
            grouped = keep.tile([P, HALF, PACK], BF16, name=f"grouped{h}", align_bytes=64)
            for copy, cols in ((nc.scalar.copy, slice(0, act_cols)), (nc.vector.tensor_copy, slice(act_cols, HALF))):
                if cols.stop > cols.start:
                    copy(
                        out=grouped[:, cols, :].rearrange("p (c i) t -> p c t i", i=4),
                        in_=raw[h][:, :, cols].rearrange("p t (c i) -> p c t i", i=4),
                    )
            if h == 0:
                place_token_scales()
            sx_codes = keep.tile([P, HALF], U32, name=f"sx_codes{h}", align_bytes=64)
            sx_plane = keep.tile([P, HALF], U8, name=f"sx_plane{h}", align_bytes=64)
            nc.vector.quantize_mx(
                out=sx_codes[:].bitcast(FP8X4), scales=sx_plane[:], in_=grouped[:].rearrange("p j t -> p (j t)")
            )
            quantised[h] = (sx_codes, sx_plane)

        def gate_pair(h, u, bank_tag, pieces):
            sx_codes, sx_plane = quantised[h]
            if True:
                q_bank = psum.tile([P, 2, HALF], F32, name=f"q{h}{u}", tag=bank_tag)
                for i in range(2):
                    cols = slice((2 * u + i) * P, (2 * u + i + 1) * P)
                    nc.tensor.matmul_mx(out=q_bank[:, i, :], lhsT=ws_codes[:, cols].bitcast(FP8X4), lhsT_scale=ws_plane[:, cols], rhs=sx_codes[:].bitcast(FP8X4), rhs_scale=sx_plane[:], start=True, stop=True)
                gate = keep.tile([P, 2, HALF], F32, name=f"gate{h}{u}")
                for i0, i1 in pieces:
                    nc.scalar.activation(out=gate[:, i0:i1, :], in_=q_bank[:, i0:i1, :], func=mybir.ActivationFunctionType.Sigmoid)
                gates[h, u] = gate

        def pick_half(h):
            picked[h] = keep.tile([P, HALF], U32, name=f"xw_picked{h}", align_bytes=64)
            nc.vector.tensor_copy(
                picked[h][:], xw_window[:].bitcast(U32).indirect(lists[:, h * (HALF // 16) : (h + 1) * (HALF // 16)])
            )

        def product(h, ms, tag):
            bank = psum.tile([P, len(ms), HALF], F32, name=f"p{h}{ms[0]}", tag=tag)
            for i, m in enumerate(ms):
                nc.tensor.matmul_mx(out=bank[:, i, :], lhsT=w_codes[:, 2 * m * P : 2 * (m + 1) * P].bitcast(FP4X4), lhsT_scale=w_plane[:, m * P : (m + 1) * P], rhs=picked[h][:].bitcast(FP8X4), rhs_scale=x_plane[:, h * HALF : (h + 1) * HALF], start=True, stop=True)
            for i, m in enumerate(ms):
                p_banks[h, m] = (bank, i)

        def finish(h, ms):
            m0, count = ms[0], len(ms)
            result = keep.tile([P, count, HALF], F32, name=f"result{h}{m0}")
            bank, i0 = p_banks[h, m0]
            gate = gates[h, m0 // 2][:, m0 % 2 : m0 % 2 + count, :]
            nc.vector.tensor_tensor(out=result[:], in0=bank[:, i0 : i0 + count, :], in1=gate, op=mybir.AluOpType.mult)
            nc.sync.dma_start(out=out_rows[:, m0 : m0 + count, h * HALF : (h + 1) * HALF], in_=result[:])

        whole = [(0, 2)]
        for h in range(2):
            gate_half(h, 0)
            for u in range(2):
                gate_pair(h, u, f"q{u}", whole)
        pick_half(0)
        pick_half(1)
        pieces = [(0, [0]), (0, [1]), (0, [2, 3]), (1, [0, 1]), (1, [2]), (1, [3])]
        for h, ms in pieces:
            product(h, ms, f"p{h}{ms[0]}")
        for h, ms in [(0, [0]), (0, [1]), (0, [2]), (0, [3]), (1, [0, 1]), (1, [2]), (1, [3])]:
            finish(h, ms)
